import numpy as np
CORES = [2,3,10,11,18,19,26,27,34,35,42,43,50,51,58,59]
N = 16
WIDTHS = [32,8,0,32,0,0,32,16,8,4,8,64,8,0,4,0]
OFF = [0,32,40,40,72,72,72,104,120,128,132,140,204,212,212,216]
C = 216
def setup_inputs(rng):
    return {"x": rng.standard_normal((N, 128, C), dtype=np.float32)}
def reference(x):
    s = x.sum(axis=0, dtype=np.float64).astype(x.dtype)
    YW = max(WIDTHS)
    y = np.full((N, 128, YW), np.nan, x.dtype)
    for r in range(N):
        y[r][:, :WIDTHS[r]] = s[:, OFF[r]:OFF[r] + WIDTHS[r]]
    return {"y": y}

@@ -1,0 +1,112 @@
+from concourse.bass import DstId, RemoteDMATransfer
+
+C_MAX = 216
+SCRATCH = {
+    "xs": ("sbuf", [128, C_MAX], "float32"),
+    "xa": ("sbuf", [128, C_MAX], "float32"),
+    "xb": ("sbuf", [128, C_MAX], "float32"),
+    "m": ("sbuf", [128, C_MAX], "float32"),
+    "sw0": ("sbuf", [128, C_MAX], "float32"),
+    "sw1": ("sbuf", [128, C_MAX], "float32"),
+    "sw2": ("sbuf", [128, C_MAX], "float32"),
+    "sw3": ("sbuf", [128, C_MAX], "float32"),
+    "fin": ("sbuf", [128, C_MAX], "float32"),
+}
+SEMAPHORES = ["loaded", "s1", "s2", "s3", "s4", "sent", "stored"]
+
+
+def runs(keys):
+    out = []
+    a = 0
+    for j in range(1, len(keys) + 1):
+        if j == len(keys) or keys[j] != keys[a]:
+            out.append((a, j, keys[a]))
+            a = j
+    return out
+
+
+def plan(T):
+    W = T.tables["WIDTHS"]
+    O = T.tables["OFF"]
+    C = T.tables["C"]
+    owner = [None] * C
+    for r, c in enumerate(T.cores):
+        for j in range(O[r], O[r] + W[r]):
+            owner[j] = c
+    lane = [None] * C
+    flip = 0
+    for (a, b, ch) in runs([o // 8 for o in owner]):
+        mid = (a + b) // 2
+        for j in range(a, b):
+            die1 = (j < mid) != bool(flip)
+            lane[j] = (5 - owner[j] % 8) if die1 else 6
+        flip ^= 1
+    return owner, lane
+
+
+def rank_program(g, core, T, topo):
+    owner, lane = plan(T)
+    C = len(owner)
+    ch, k = core // 8, core % 8
+    par = ch & 1
+    if k not in (2, 3, 6):
+        return
+    rank = T.rank_of(core)
+    sent = 0
+
+    def fold(srcs, dst_core, dst_ap, sem):
+        rid, pid, _se = topo.addr(dst_core)
+        mask = topo.mask(core, dst_core)
+        g.remote_dma_fused([RemoteDMATransfer(dst_ids=[DstId(rid=rid, pnc=pid)], dma_engine_mask=mask,
+                                              remote_sem=sem, srcs=srcs, dsts=[dst_ap], alu_op=1)],
+                           local_sem=T.sem.sent)
+        return 16 if mask == 0xFFFF else 8
+
+    lane_runs = runs(lane)
+    if rank is not None:
+        g.sync.dma_start(T.xs[:], T.x[:]).then_inc(T.sem.loaded, 16)
+        g.wait_ge(T.sem.loaded, 16)
+        land = T.xa if k == 2 else T.xb
+        for (a, b, L) in lane_runs:
+            if L != k:
+                rid, pid, _se = topo.addr(ch * 8 + L)
+                g.remote_dma(land[:, a:b], T.xs[:, a:b], T.sem.s1, T.sem.sent, pid, rid, 0xFFFF)
+                sent += 16
+
+    A = T.xs if k == 2 else T.xa
+    B = T.xs if k == 3 else T.xb
+    n1 = sum(1 for (a, b, L) in lane_runs if L == k) * (1 if rank is not None else 2)
+    g.wait_ge(T.sem.s1, 16 * n1)
+
+    r2 = runs([(lane[j], (owner[j] // 8) & 1) for j in range(C)])
+    for (a, b, (L, p)) in r2:
+        if L == k and p != par:
+            sent += fold([A[:, a:b], B[:, a:b]], (ch ^ 1) * 8 + k, T.m[:, a:b], T.sem.s2)
+    n2 = sum(1 for (a, b, (L, p)) in r2 if L == k and p == par)
+    g.wait_ge(T.sem.s2, 8 * n2)
+
+    r3 = runs([(lane[j], owner[j] // 8) for j in range(C)])
+    for (a, b, (L, d)) in r3:
+        if L == k and (d & 1) == par and d != ch:
+            sent += fold([A[:, a:b], B[:, a:b], T.m[:, a:b]], d * 8 + k, T["sw%d" % (ch // 2)][:, a:b], T.sem.s3)
+    n3 = sum(1 for (a, b, (L, d)) in r3 if L == k and d == ch)
+    if n3:
+        g.wait_ge(T.sem.s3, 8 * 3 * n3)
+
+    r4 = runs([(lane[j], owner[j]) for j in range(C)])
+    for (a, b, (L, o)) in r4:
+        if L == k and o // 8 == ch:
+            srcs = [A[:, a:b], B[:, a:b], T.m[:, a:b]]
+            srcs += [T["sw%d" % q][:, a:b] for q in range(4) if q != ch // 2]
+            sent += fold(srcs, o, T.fin[:, a:b], T.sem.s4)
+    if rank is not None:
+        n4 = sum(1 for (a, b, (L, o)) in r4 if o == core)
+        if n4:
+            g.wait_ge(T.sem.s4, 16 * n4)
+            w = T.tables["WIDTHS"][rank]
+            off = T.tables["OFF"][rank]
+            g.sync.wait_ge(T.sem.s4, 16 * n4)
+            g.sync.dma_start(T.y[:, 0:w], T.fin[:, off:off + w]).then_inc(T.sem.stored, 16)
+            g.wait_ge(T.sem.stored, 16)
+    if sent:
+        g.wait_ge(T.sem.sent, sent)

@@ -1,112 +1,123 @@
 from concourse.bass import DstId, RemoteDMATransfer
 
-C_MAX = 216
-SCRATCH = {
-    "xs": ("sbuf", [128, C_MAX], "float32"),
-    "xa": ("sbuf", [128, C_MAX], "float32"),
-    "xb": ("sbuf", [128, C_MAX], "float32"),
-    "m": ("sbuf", [128, C_MAX], "float32"),
-    "sw0": ("sbuf", [128, C_MAX], "float32"),
-    "sw1": ("sbuf", [128, C_MAX], "float32"),
-    "sw2": ("sbuf", [128, C_MAX], "float32"),
-    "sw3": ("sbuf", [128, C_MAX], "float32"),
-    "fin": ("sbuf", [128, C_MAX], "float32"),
-}
-SEMAPHORES = ["loaded", "s1", "s2", "s3", "s4", "sent", "stored"]
+PIECES = [(0, 40, 0), (40, 72, 1), (72, 96, 3), (96, 120, 3), (120, 132, 4),
+          (132, 168, 5), (168, 204, 5), (204, 212, 6), (212, 216, 7)]
+PARENT = [[-1, 0, 0, 2, 6, 1, 0, 6],
+          [1, -1, 0, 7, 0, 1, 7, 1],
+          [2, 3, 3, -1, 2, 1, 2, 3],
+          [2, 7, 3, -1, 2, 7, 2, 3],
+          [6, 5, 4, 2, -1, 4, 4, 6],
+          [4, 3, 4, 5, 5, -1, 4, 3],
+          [1, 5, 4, 7, 5, -1, 7, 5],
+          [6, 0, 6, 7, 6, 4, -1, 6],
+          [6, 5, 6, 5, 6, 7, 7, -1]]
+HANDLER = [[0, 3, 2, 3, 3, 6, 4, 3],
+           [2, 2, 5, 2, 0, 2, 6, 5],
+           [4, 4, 3, 0, 4, 0, 0, 0],
+           [1, 1, 6, 5, 5, 7, 2, 2],
+           [5, 3, 7, 7, 1, 2, 1, 6],
+           [3, 5, 4, 4, 2, 5, 5, 3],
+           [6, 0, 0, 6, 6, 4, 2, 4],
+           [7, 6, 1, 1, 7, 7, 3, 7],
+           [5, 1, 7, 1, 7, 1, 7, 1]]
+NP = len(PIECES)
+NCHIPS = 8
+KIDS = [[[c for c in range(NCHIPS) if PARENT[q][c] == p] for p in range(NCHIPS)] for q in range(NP)]
+CHIP_LO = [min([a for (a, b, d) in PIECES if d == c] + [10 ** 9]) for c in range(NCHIPS)]
+CHIP_HI = [max([b for (a, b, d) in PIECES if d == c] + [0]) for c in range(NCHIPS)]
+
+SCRATCH = {"fin": ("sbuf", [128, max(CHIP_HI[c] - CHIP_LO[c] for c in range(NCHIPS))], "float32")}
+for _q in range(NP):
+    SCRATCH["p%d" % _q] = ("dram", [2 + max(len(k) for k in KIDS[_q]), 128, PIECES[_q][1] - PIECES[_q][0]], "float32")
+SEMAPHORES = ["n%d" % _q for _q in range(NP)] + ["fin", "sent", "stored"]
 
 
-def runs(keys):
-    out = []
-    a = 0
-    for j in range(1, len(keys) + 1):
-        if j == len(keys) or keys[j] != keys[a]:
-            out.append((a, j, keys[a]))
-            a = j
-    return out
+def depth(q, c):
+    n = 0
+    while PARENT[q][c] >= 0:
+        c = PARENT[q][c]
+        n += 1
+    return n
 
 
-def plan(T):
-    W = T.tables["WIDTHS"]
-    O = T.tables["OFF"]
-    C = T.tables["C"]
-    owner = [None] * C
-    for r, c in enumerate(T.cores):
-        for j in range(O[r], O[r] + W[r]):
-            owner[j] = c
-    lane = [None] * C
-    flip = 0
-    for (a, b, ch) in runs([o // 8 for o in owner]):
-        mid = (a + b) // 2
-        for j in range(a, b):
-            die1 = (j < mid) != bool(flip)
-            lane[j] = (5 - owner[j] % 8) if die1 else 6
-        flip ^= 1
-    return owner, lane
+def height(q, c):
+    return 1 + max(height(q, k) for k in KIDS[q][c]) if KIDS[q][c] else 0
+
+
+def engines(mask):
+    return bin(mask).count("1")
+
+
+def check_plan(T, topo):
+    W, O = T.tables["WIDTHS"], T.tables["OFF"]
+    assert PIECES[0][0] == 0 and PIECES[-1][1] == T.tables["C"]
+    for q, (a, b, d) in enumerate(PIECES):
+        assert q == 0 or PIECES[q - 1][1] == a
+        own = [r for r, c in enumerate(T.cores) if O[r] < b and a < O[r] + W[r]]
+        assert own and all(T.cores[r] // 8 == d for r in own)
+        assert all(T.cores[r] != d * 8 + HANDLER[q][d] for r in own)
+        for c in range(NCHIPS):
+            p = PARENT[q][c]
+            assert (p < 0) == (c == d) and depth(q, c) <= 2
+            if p >= 0:
+                assert topo.mates(c, p) or topo.same_plane(c, p)
+                assert topo.may_write(c * 8 + HANDLER[q][c], p * 8 + HANDLER[q][p])
 
 
 def rank_program(g, core, T, topo):
-    owner, lane = plan(T)
-    C = len(owner)
+    check_plan(T, topo)
+    W, O = T.tables["WIDTHS"], T.tables["OFF"]
     ch, k = core // 8, core % 8
-    par = ch & 1
-    if k not in (2, 3, 6):
-        return
     rank = T.rank_of(core)
+    chip_ranks = [c for c in T.cores if c // 8 == ch]
     sent = 0
 
-    def fold(srcs, dst_core, dst_ap, sem):
-        rid, pid, _se = topo.addr(dst_core)
-        mask = topo.mask(core, dst_core)
-        g.remote_dma_fused([RemoteDMATransfer(dst_ids=[DstId(rid=rid, pnc=pid)], dma_engine_mask=mask,
-                                              remote_sem=sem, srcs=srcs, dsts=[dst_ap], alu_op=1)],
-                           local_sem=T.sem.sent)
-        return 16 if mask == 0xFFFF else 8
-
-    lane_runs = runs(lane)
     if rank is not None:
-        g.sync.dma_start(T.xs[:], T.x[:]).then_inc(T.sem.loaded, 16)
-        g.wait_ge(T.sem.loaded, 16)
-        land = T.xa if k == 2 else T.xb
-        for (a, b, L) in lane_runs:
-            if L != k:
-                rid, pid, _se = topo.addr(ch * 8 + L)
-                g.remote_dma(land[:, a:b], T.xs[:, a:b], T.sem.s1, T.sem.sent, pid, rid, 0xFFFF)
-                sent += 16
+        slot = chip_ranks.index(core)
+        order = sorted(range(NP), key=lambda q: -depth(q, ch))
+        for i, q in enumerate(order):
+            a, b, _d = PIECES[q]
+            queue = g.sync if i % 2 == 0 else g.scalar
+            queue.dma_start(T["p%d" % q][slot], T.x[:, a:b]).then_inc(T.sem["n%d" % q], 16)
+        for q in order:
+            h = ch * 8 + HANDLER[q][ch]
+            if h != core:
+                rid, pid, _se = topo.addr(h)
+                mask = topo.mask(core, h)
+                g.wait_ge(T.sem["n%d" % q], 16)
+                g.remote_dma(T["p%d" % q][slot], T["p%d" % q][slot], T.sem["n%d" % q], T.sem.sent, pid, rid, mask)
+                sent += engines(mask)
 
-    A = T.xs if k == 2 else T.xa
-    B = T.xs if k == 3 else T.xb
-    n1 = sum(1 for (a, b, L) in lane_runs if L == k) * (1 if rank is not None else 2)
-    g.wait_ge(T.sem.s1, 16 * n1)
+    mine = [q for q in range(NP) if HANDLER[q][ch] == k]
+    mine.sort(key=lambda q: (height(q, ch), -depth(q, ch)))
+    for q in mine:
+        a, b, d = PIECES[q]
+        buf = T["p%d" % q]
+        kids = KIDS[q][ch]
+        g.wait_ge(T.sem["n%d" % q], 16 * len(chip_ranks) + 8 * len(kids))
+        srcs = [buf[i] for i in range(len(chip_ranks) + len(kids))]
+        if ch != d:
+            p = PARENT[q][ch]
+            dst = p * 8 + HANDLER[q][p]
+            rid, pid, _se = topo.addr(dst)
+            mask = topo.mask(core, dst)
+            tr = RemoteDMATransfer(dst_ids=[DstId(rid=rid, pnc=pid)], dma_engine_mask=mask,
+                                   remote_sem=T.sem["n%d" % q], srcs=srcs,
+                                   dsts=[buf[2 + KIDS[q][p].index(ch)]], alu_op=1)
+        else:
+            owners = [c for r, c in enumerate(T.cores) if O[r] < b and a < O[r] + W[r]]
+            mask = 0xFFFF
+            ids = [DstId(rid=topo.addr(c)[0], pnc=topo.addr(c)[1]) for c in owners]
+            tr = RemoteDMATransfer(dst_ids=ids, dma_engine_mask=mask, remote_sem=T.sem.fin, srcs=srcs,
+                                   dsts=[T.fin[:, a - CHIP_LO[d]:b - CHIP_LO[d]] for _c in owners], alu_op=1)
+        g.remote_dma_fused([tr], local_sem=T.sem.sent)
+        sent += engines(mask)
 
-    r2 = runs([(lane[j], (owner[j] // 8) & 1) for j in range(C)])
-    for (a, b, (L, p)) in r2:
-        if L == k and p != par:
-            sent += fold([A[:, a:b], B[:, a:b]], (ch ^ 1) * 8 + k, T.m[:, a:b], T.sem.s2)
-    n2 = sum(1 for (a, b, (L, p)) in r2 if L == k and p == par)
-    g.wait_ge(T.sem.s2, 8 * n2)
-
-    r3 = runs([(lane[j], owner[j] // 8) for j in range(C)])
-    for (a, b, (L, d)) in r3:
-        if L == k and (d & 1) == par and d != ch:
-            sent += fold([A[:, a:b], B[:, a:b], T.m[:, a:b]], d * 8 + k, T["sw%d" % (ch // 2)][:, a:b], T.sem.s3)
-    n3 = sum(1 for (a, b, (L, d)) in r3 if L == k and d == ch)
-    if n3:
-        g.wait_ge(T.sem.s3, 8 * 3 * n3)
-
-    r4 = runs([(lane[j], owner[j]) for j in range(C)])
-    for (a, b, (L, o)) in r4:
-        if L == k and o // 8 == ch:
-            srcs = [A[:, a:b], B[:, a:b], T.m[:, a:b]]
-            srcs += [T["sw%d" % q][:, a:b] for q in range(4) if q != ch // 2]
-            sent += fold(srcs, o, T.fin[:, a:b], T.sem.s4)
-    if rank is not None:
-        n4 = sum(1 for (a, b, (L, o)) in r4 if o == core)
-        if n4:
-            g.wait_ge(T.sem.s4, 16 * n4)
-            w = T.tables["WIDTHS"][rank]
-            off = T.tables["OFF"][rank]
-            g.sync.wait_ge(T.sem.s4, 16 * n4)
-            g.sync.dma_start(T.y[:, 0:w], T.fin[:, off:off + w]).then_inc(T.sem.stored, 16)
-            g.wait_ge(T.sem.stored, 16)
+    if rank is not None and W[rank]:
+        lo, hi = O[rank], O[rank] + W[rank]
+        n = sum(1 for (a, b, _d) in PIECES if lo < b and a < hi)
+        g.sync.wait_ge(T.sem.fin, 16 * n)
+        g.sync.dma_start(T.y[:, 0:W[rank]], T.fin[:, lo - CHIP_LO[ch]:hi - CHIP_LO[ch]]).then_inc(T.sem.stored, 16)
+        g.wait_ge(T.sem.stored, 16)
     if sent:
         g.wait_ge(T.sem.sent, sent)

from concourse.bass import DstId, RemoteDMATransfer

PIECES = [(0, 40, 0), (40, 72, 1), (72, 96, 3), (96, 120, 3), (120, 132, 4),
          (132, 168, 5), (168, 204, 5), (204, 212, 6), (212, 216, 7)]
PARENT = [[-1, 0, 0, 2, 6, 1, 0, 6],
          [1, -1, 0, 7, 0, 1, 7, 1],
          [2, 3, 3, -1, 2, 1, 2, 3],
          [2, 7, 3, -1, 2, 7, 2, 3],
          [6, 5, 4, 2, -1, 4, 4, 6],
          [4, 3, 4, 5, 5, -1, 4, 3],
          [1, 5, 4, 7, 5, -1, 7, 5],
          [6, 0, 6, 7, 6, 4, -1, 6],
          [6, 5, 6, 5, 6, 7, 7, -1]]
HANDLER = [[0, 3, 2, 3, 3, 6, 4, 3],
           [2, 2, 5, 2, 0, 2, 6, 5],
           [4, 4, 3, 0, 4, 0, 0, 0],
           [1, 1, 6, 5, 5, 7, 2, 2],
           [5, 3, 7, 7, 1, 2, 1, 6],
           [3, 5, 4, 4, 2, 5, 5, 3],
           [6, 0, 0, 6, 6, 4, 2, 4],
           [7, 6, 1, 1, 7, 7, 3, 7],
           [5, 1, 7, 1, 7, 1, 7, 1]]
NP = len(PIECES)
NCHIPS = 8
KIDS = [[[c for c in range(NCHIPS) if PARENT[q][c] == p] for p in range(NCHIPS)] for q in range(NP)]
CHIP_LO = [min([a for (a, b, d) in PIECES if d == c] + [10 ** 9]) for c in range(NCHIPS)]
CHIP_HI = [max([b for (a, b, d) in PIECES if d == c] + [0]) for c in range(NCHIPS)]

SCRATCH = {"fin": ("sbuf", [128, max(CHIP_HI[c] - CHIP_LO[c] for c in range(NCHIPS))], "float32")}
for _q in range(NP):
    SCRATCH["p%d" % _q] = ("dram", [2 + max(len(k) for k in KIDS[_q]), 128, PIECES[_q][1] - PIECES[_q][0]], "float32")
SEMAPHORES = ["n%d" % _q for _q in range(NP)] + ["fin", "sent", "stored"]


def depth(q, c):
    n = 0
    while PARENT[q][c] >= 0:
        c = PARENT[q][c]
        n += 1
    return n


def height(q, c):
    return 1 + max(height(q, k) for k in KIDS[q][c]) if KIDS[q][c] else 0


def engines(mask):
    return bin(mask).count("1")


def check_plan(T, topo):
    W, O = T.tables["WIDTHS"], T.tables["OFF"]
    assert PIECES[0][0] == 0 and PIECES[-1][1] == T.tables["C"]
    for q, (a, b, d) in enumerate(PIECES):
        assert q == 0 or PIECES[q - 1][1] == a
        own = [r for r, c in enumerate(T.cores) if O[r] < b and a < O[r] + W[r]]
        assert own and all(T.cores[r] // 8 == d for r in own)
        assert all(T.cores[r] != d * 8 + HANDLER[q][d] for r in own)
        for c in range(NCHIPS):
            p = PARENT[q][c]
            assert (p < 0) == (c == d) and depth(q, c) <= 2
            if p >= 0:
                assert topo.mates(c, p) or topo.same_plane(c, p)
                assert topo.may_write(c * 8 + HANDLER[q][c], p * 8 + HANDLER[q][p])


def rank_program(g, core, T, topo):
    check_plan(T, topo)
    W, O = T.tables["WIDTHS"], T.tables["OFF"]
    ch, k = core // 8, core % 8
    rank = T.rank_of(core)
    chip_ranks = [c for c in T.cores if c // 8 == ch]
    sent = 0

    if rank is not None:
        slot = chip_ranks.index(core)
        order = sorted(range(NP), key=lambda q: -depth(q, ch))
        for i, q in enumerate(order):
            a, b, _d = PIECES[q]
            queue = g.sync if i % 2 == 0 else g.scalar
            queue.dma_start(T["p%d" % q][slot], T.x[:, a:b]).then_inc(T.sem["n%d" % q], 16)
        for q in order:
            h = ch * 8 + HANDLER[q][ch]
            if h != core:
                rid, pid, _se = topo.addr(h)
                mask = topo.mask(core, h)
                g.wait_ge(T.sem["n%d" % q], 16)
                g.remote_dma(T["p%d" % q][slot], T["p%d" % q][slot], T.sem["n%d" % q], T.sem.sent, pid, rid, mask)
                sent += engines(mask)

    mine = [q for q in range(NP) if HANDLER[q][ch] == k]
    mine.sort(key=lambda q: (height(q, ch), -depth(q, ch)))
    for q in mine:
        a, b, d = PIECES[q]
        buf = T["p%d" % q]
        kids = KIDS[q][ch]
        g.wait_ge(T.sem["n%d" % q], 16 * len(chip_ranks) + 8 * len(kids))
        srcs = [buf[i] for i in range(len(chip_ranks) + len(kids))]
        if ch != d:
            p = PARENT[q][ch]
            dst = p * 8 + HANDLER[q][p]
            rid, pid, _se = topo.addr(dst)
            mask = topo.mask(core, dst)
            tr = RemoteDMATransfer(dst_ids=[DstId(rid=rid, pnc=pid)], dma_engine_mask=mask,
                                   remote_sem=T.sem["n%d" % q], srcs=srcs,
                                   dsts=[buf[2 + KIDS[q][p].index(ch)]], alu_op=1)
        else:
            owners = [c for r, c in enumerate(T.cores) if O[r] < b and a < O[r] + W[r]]
            mask = 0xFFFF
            ids = [DstId(rid=topo.addr(c)[0], pnc=topo.addr(c)[1]) for c in owners]
            tr = RemoteDMATransfer(dst_ids=ids, dma_engine_mask=mask, remote_sem=T.sem.fin, srcs=srcs,
                                   dsts=[T.fin[:, a - CHIP_LO[d]:b - CHIP_LO[d]] for _c in owners], alu_op=1)
        g.remote_dma_fused([tr], local_sem=T.sem.sent)
        sent += engines(mask)

    if rank is not None and W[rank]:
        lo, hi = O[rank], O[rank] + W[rank]
        n = sum(1 for (a, b, _d) in PIECES if lo < b and a < hi)
        g.sync.wait_ge(T.sem.fin, 16 * n)
        g.sync.dma_start(T.y[:, 0:W[rank]], T.fin[:, lo - CHIP_LO[ch]:hi - CHIP_LO[ch]]).then_inc(T.sem.stored, 16)
        g.wait_ge(T.sem.stored, 16)
    if sent:
        g.wait_ge(T.sem.sent, sent)
